import numpy as np
import ml_dtypes


def mxq(x, axis, fmt="e4m3"):
    dtype, down = {"e4m3": (ml_dtypes.float8_e4m3fn, 7), "e5m2": (ml_dtypes.float8_e5m2, 14)}[fmt]
    v = np.moveaxis(np.asarray(x, np.float32).astype(ml_dtypes.bfloat16).astype(np.float64), axis, -1)
    blocks = v.reshape(v.shape[:-1] + (-1, 32))
    amax = np.abs(blocks).max(-1, keepdims=True)
    byte = np.maximum(np.where(amax > 0, np.frexp(amax)[1] - 1 + 127, 0) - down, 1)
    scale = np.exp2(byte - 127.0)
    codes = (blocks / scale).astype(np.float32).astype(dtype).astype(np.float64)
    return np.moveaxis((codes * scale).reshape(v.shape), -1, axis)


WIDE = False


def mx_kscale(k):
    if not WIDE:
        return np.ones(k)
    levels = np.array([10, -10, 5, -5, 0])
    if k % 512:
        return np.exp2(np.random.permutation(np.resize(levels, k // 32))).repeat(32)
    a = np.empty((k // 512, 16))
    for p in range(k // 512):
        a[p, :8] = np.random.permutation(np.resize(levels, 8))
        for g in range(8):
            far = levels[np.abs(levels - a[p, g]) >= 10]
            a[p, g + 8] = far[np.random.randint(len(far))]
    return np.exp2(a.ravel()).repeat(32)


def f64(x):
    return np.asarray(x).astype(np.float64)


def striped(idx):
    return np.tile(idx.reshape(-1, 16).T, (8, 1)).astype(np.uint16)


def unstriped(offs):
    return offs[:16].T.reshape(-1).astype(np.int64)


def pack_weight(w):
    k, n = w.shape
    w = f64(np.asarray(w, np.float32).astype(ml_dtypes.bfloat16)).reshape(k // 32, 32, n)
    amax = np.abs(w).max(1)
    byte = np.clip(np.where(amax > 0, np.frexp(amax)[1] - 1 + 127 - 7, 1), 1, 254)
    scaled = (w * np.exp2(127.0 - byte)[:, None, :]).reshape(k, n).astype(np.float32)
    words = np.ascontiguousarray(scaled.reshape(k // 512, 128, 4, n).transpose(0, 1, 3, 2)).astype(ml_dtypes.float8_e4m3fn).view(np.uint8)
    return words, np.ascontiguousarray(byte.astype(np.uint8).reshape(k // 512, 16, n))


def unpack_weight(words, scales):
    g, p, n, _ = words.shape
    vals = np.ascontiguousarray(words).view(ml_dtypes.float8_e4m3fn).astype(np.float64) * np.repeat(np.exp2(scales.astype(np.float64) - 127.0), 8, axis=1)[..., None]
    return vals.transpose(0, 1, 3, 2).reshape(g * 512, n)


E2M1 = np.array([0.0, 0.5, 1.0, 1.5, 2.0, 3.0, 4.0, 6.0, -0.0, -0.5, -1.0, -1.5, -2.0, -3.0, -4.0, -6.0])


def pack_fp4(w):
    k, n = w.shape
    w = f64(np.asarray(w, np.float32).astype(ml_dtypes.bfloat16)).reshape(k // 32, 32, n)
    amax = np.abs(w).max(1)
    mant, ex = np.frexp(amax / 6.0)
    byte = np.clip(np.where(amax > 0, np.where(mant > 0.5, ex, ex - 1) + 127, 1), 1, 254)
    scaled = (w * np.exp2(127.0 - byte)[:, None, :]).reshape(k, n).astype(np.float32)
    c = np.ascontiguousarray(scaled.reshape(k // 512, 128, 4, n).transpose(0, 1, 3, 2)).astype(ml_dtypes.float4_e2m1fn).view(np.uint8) & 0xF
    words = (c[..., 0::2] | (c[..., 1::2] << 4)).reshape(k // 512, 128, 2 * n)
    return np.ascontiguousarray(words), np.ascontiguousarray(byte.astype(np.uint8).reshape(k // 512, 16, n))


def unpack_fp4(words, scales):
    g, _, n = scales.shape
    words = np.ascontiguousarray(words).reshape(g, 128, n, 2)
    nib = np.empty((g, 128, n, 4), np.uint8)
    nib[..., 0::2] = words & 0xF
    nib[..., 1::2] = words >> 4
    vals = E2M1[nib] * np.repeat(np.exp2(scales.astype(np.float64) - 127.0), 8, axis=1)[..., None]
    return vals.transpose(0, 1, 3, 2).reshape(g * 512, n)


def relu(v):
    return np.maximum(v, 0.0)


K, T, S, N, H = 1024, 1024, 512, 128, 512


def setup_inputs():
    n = np.random.standard_normal
    s = mx_kscale(K)[:, None]
    u = mx_kscale(H)
    packed_xT = pack_weight(n((K, T)) * s)
    packed_w1 = pack_fp4(n((K, H)) / np.sqrt(K) / s)
    packed_w2 = pack_fp4(n((K, H)) / np.sqrt(K) / s)
    packed_w3 = pack_fp4(n((H, N)) / np.sqrt(H) / u[:, None])
    return {
        "x_words": packed_xT[0],
        "x_scales": packed_xT[1],
        "w1_words": packed_w1[0],
        "w1_scales": packed_w1[1],
        "w2_words": packed_w2[0],
        "w2_scales": packed_w2[1],
        "kap": (np.random.uniform(0.7, 1.5, (H, 1))).astype(np.float32),
        "z2": (0.8 * n((H, S))).astype(np.float32),
        "unit": (np.random.uniform(0.6, 1.4, (H, 1)) * u[:, None]).astype(np.float32),
        "w3_words": packed_w3[0],
        "w3_scales": packed_w3[1],
        "offs": striped(np.random.permutation(T)[:S]),
        "anti": striped(np.random.permutation(S)),
    }


def reference(x_words, x_scales, w1_words, w1_scales, w2_words, w2_scales, kap, z2, unit, w3_words, w3_scales, offs, anti):
    xq = unpack_weight(x_words, x_scales)[:, unstriped(offs)]
    vv = unpack_fp4(w1_words, w1_scales).T @ xq
    var = np.log(np.exp(vv) + 1.0)
    vol = np.sqrt(var + 0.02)
    dw = unpack_fp4(w2_words, w2_scales).T @ xq
    vnew = relu(var + f64(kap) * (-1.0 * var + 0.7) + 0.4 * (vol * dw))
    ret = -0.25 * (var + vnew) + vol * (-0.5 * dw + f64(z2))
    spot = np.exp(0.9 * np.tanh(ret))
    va = vnew[:, unstriped(anti)]
    hid = f64(unit) * (relu(spot - 0.8) - (0.5 * va))
    return unpack_fp4(w3_words, w3_scales).T @ mxq(hid, 0, "e4m3")

@@ -1,0 +1,229 @@
+from contextlib import ExitStack
+
+import concourse.mybir as mybir
+
+K, T, S, N, H = 1024, 1024, 512, 128, 512
+FLOPS = 2 * (2 * K * H * S + H * N * S)
+
+F32 = mybir.dt.float32
+BF16 = mybir.dt.bfloat16
+I32 = mybir.dt.int32
+U32 = mybir.dt.uint32
+U16 = mybir.dt.uint16
+U8 = mybir.dt.uint8
+FP8X4 = mybir.dt.float8_e4m3fn_x4
+FP4X4 = mybir.dt.float4_e2m1fn_x4
+ALU = mybir.AluOpType
+ACT = mybir.ActivationFunctionType
+
+P = 128
+PACK = 4
+PASSES = K // (P * PACK)
+HALF = S // 2
+CHUNK = 128
+
+
+def tile_picked_yhestm_call_p_kernel(
+    tc, x_words, x_scales, w1_words, w1_scales, w2_words, w2_scales, kap, z2, unit, w3_words, w3_scales, offs, anti, out
+):
+    nc = tc.nc
+    with ExitStack() as ctx:
+        keep = ctx.enter_context(tc.tile_pool(name="keep", bufs=1))
+        psum = ctx.enter_context(tc.psum_pool(name="psum", bufs=1))
+
+        def sb(shape, dtype, name, tag=None):
+            return keep.tile(shape, dtype, name=name, tag=tag or name, align_bytes=64)
+
+        offs_sb = keep.tile([P, S // 16], U16, name="offs_sb")
+        anti_sb = keep.tile([P, S // 16], U16, name="anti_sb")
+        xs = sb([P, PASSES, T], U8, "xs")
+        w1s_raw = sb([P, PASSES, H], U8, "w1s_raw")
+        w2s_raw = sb([P, PASSES, H], U8, "w2s_raw")
+        nc.gpsimd.memset(xs[:].bitcast(I32), 0)
+        nc.vector.memset(w1s_raw[:].bitcast(I32), 0)
+        nc.vector.memset(w2s_raw[:].bitcast(I32), 0)
+
+        def load_scales(queues, tile, dram):
+            for q, queue in enumerate(queues):
+                queue.dma_start(
+                    out=tile[32 * q : 32 * q + 4, :, :].bitcast(I32),
+                    in_=dram[:, 4 * q : 4 * q + 4, :].rearrange("o r n -> r o n").bitcast(I32),
+                )
+
+        xw = sb([P, PASSES, T], U32, "xw")
+        w1_raw = sb([P, PASSES, 2 * H], U8, "w1_raw")
+
+        nc.sync.dma_start(offs_sb[:], offs)
+        load_scales([nc.sync] * 4, xs, x_scales)
+        nc.scalar.dma_start(out=w1_raw[:].bitcast(I32), in_=w1_words.rearrange("o p n -> p o n").bitcast(I32))
+        nc.scalar.dma_start(out=xw[:].bitcast(I32), in_=x_words.rearrange("o p n t -> p o (n t)").bitcast(I32))
+        nc.sync.dma_start(anti_sb[:], anti)
+        load_scales([nc.gpsimd, nc.gpsimd, nc.sync, nc.sync], w1s_raw, w1_scales)
+        load_scales([nc.gpsimd, nc.gpsimd, nc.sync, nc.sync], w2s_raw, w2_scales)
+
+        def deal_words(raw, name):
+            dealt = sb([P, PASSES, 2 * H], U8, name)
+            nc.vector.tensor_copy(
+                out=dealt[:].bitcast(U16).rearrange("p o (t m) -> p o t m", t=PACK),
+                in_=raw[:].bitcast(U16).rearrange("p o (m t) -> p o t m", t=PACK),
+            )
+            return dealt
+
+        def deal_scales(raw, name):
+            dealt = sb([P, PASSES, H], U8, name)
+            nc.vector.tensor_copy(
+                out=dealt[:].rearrange("p o (t m) -> p o t m", t=PACK),
+                in_=raw[:].rearrange("p o (m t) -> p o t m", t=PACK),
+            )
+            return dealt
+
+        gw = [[sb([P, HALF], U32, f"gw{h}{o}") for o in range(PASSES)] for h in range(2)]
+        gs = [[sb([P, HALF], U8, f"gs{h}{o}") for o in range(PASSES)] for h in range(2)]
+
+        def gather_paths(h):
+            picked = offs_sb[:, h * HALF // 16 : (h + 1) * HALF // 16]
+            for o in range(PASSES):
+                nc.vector.tensor_copy(gs[h][o][:], xs[:, o, :].indirect(picked))
+            for o in range(PASSES):
+                nc.vector.tensor_copy(gw[h][o][:], xw[:, o, :].indirect(picked))
+
+        def product(words, scales, h, tp, tag):
+            bank = psum.tile([P, 2, HALF], F32, name=f"{tag}{h}{tp}", tag=f"{tag}{h}{tp}")
+            for j in range(2):
+                t = 2 * tp + j
+                for o in range(PASSES):
+                    nc.tensor.matmul_mx(
+                        out=bank[:, j, :],
+                        lhsT=words[:, o, 2 * P * t : 2 * P * (t + 1)].bitcast(FP4X4),
+                        lhsT_scale=scales[:, o, P * t : P * (t + 1)],
+                        rhs=gw[h][o][:].bitcast(FP8X4),
+                        rhs_scale=gs[h][o][:],
+                        start=(o == 0),
+                        stop=(o == PASSES - 1),
+                    )
+            return bank
+
+        def part(tile, h, tp):
+            return tile[:, 2 * tp : 2 * tp + 2, h * HALF : (h + 1) * HALF]
+
+        w1 = deal_words(w1_raw, "w1")
+        w2_raw = sb([P, PASSES, 2 * H], U8, "w2_raw", tag="w1_raw")
+        nc.sync.dma_start(out=w2_raw[:].bitcast(I32), in_=w2_words.rearrange("o p n -> p o n").bitcast(I32))
+        w1s = deal_scales(w1s_raw, "w1s")
+        gather_paths(0)
+        z2_sb = sb([P, PACK, S], F32, "z2_sb", tag="w1s_raw")
+        nc.sync.dma_start(out=z2_sb[:], in_=z2.rearrange("(p t) n -> p t n", t=PACK))
+        gather_paths(1)
+        kap_sb = sb([P, PACK], F32, "kap_sb", tag="xs")
+        unit_sb = sb([P, PACK], F32, "unit_sb", tag="xw")
+        nc.sync.dma_start(out=kap_sb[:], in_=kap.rearrange("(p t) o -> p (t o)", t=PACK))
+        nc.sync.dma_start(out=unit_sb[:], in_=unit.rearrange("(p t) o -> p (t o)", t=PACK))
+
+        def plane(name):
+            return sb([P, PACK, S], F32, name)
+
+        growth, capped, soft, var, drift, vol, shock, kick, pre, pre_anti = [
+            plane(n) for n in ("growth", "capped", "soft", "var", "drift", "vol", "shock", "kick", "pre", "pre_anti")
+        ]
+        banks = [(h, tp) for h in range(2) for tp in range(2)]
+        vv, dw = {}, {}
+        for h, tp in banks:
+            vv[h, tp] = product(w1, w1s, h, tp, "vv")
+            nc.scalar.activation(part(growth, h, tp), vv[h, tp][:], ACT.Exp)
+        w2 = deal_words(w2_raw, "w2")
+        w2s = deal_scales(w2s_raw, "w2s")
+        w3 = sb([P, 2 * N], U8, "w3", tag="w1_raw")
+        w3s = sb([P, N], U8, "w3s", tag="w2s_raw")
+        nc.gpsimd.memset(w3s[:].bitcast(I32), 0)
+        nc.sync.dma_start(out=w3[:].bitcast(I32), in_=w3_words[0].bitcast(I32))
+        for q in range(4):
+            nc.sync.dma_start(out=w3s[32 * q : 32 * q + 4, :].bitcast(I32), in_=w3_scales[0, 4 * q : 4 * q + 4, :].bitcast(I32))
+
+        half_keep = sb([P, PACK], F32, "half_keep")
+        half_pull = sb([P, PACK], F32, "half_pull")
+        neg_unit = sb([P, PACK], F32, "neg_unit")
+        nc.gpsimd.tensor_scalar(half_keep[:], kap_sb[:], -0.5, 0.5, ALU.mult, ALU.add)
+        nc.gpsimd.tensor_scalar(half_pull[:], kap_sb[:], 0.35, 0.0, ALU.mult, ALU.add)
+        nc.gpsimd.tensor_scalar(neg_unit[:], unit_sb[:], -1.0, 0.0, ALU.mult, ALU.add)
+
+        for h, tp in banks:
+            dw[h, tp] = product(w2, w2s, h, tp, "dw")
+            nc.vector.scalar_tensor_tensor(part(shock, h, tp), part(z2_sb, h, tp), -2.0, dw[h, tp][:], ALU.mult, ALU.add)
+        nc.vector.tensor_scalar(capped[:], growth[:], 2.0**60, 1.0, ALU.min, ALU.add)
+        for h in range(2):
+            cols = slice(h * HALF, (h + 1) * HALF)
+            nc.scalar.activation(soft[:, :, cols], capped[:, :, cols], ACT.Ln)
+        for h, tp in banks:
+            nc.vector.tensor_tensor(part(var, h, tp), vv[h, tp][:], part(soft, h, tp), ALU.max)
+        for h, tp in banks:
+            nc.scalar.activation(part(vol, h, tp), part(var, h, tp), ACT.Sqrt, bias=0.02)
+        for t in range(PACK):
+            if True:
+                nc.vector.tensor_scalar(drift[:, t, :], var[:, t, :], half_keep[:, t : t + 1], half_pull[:, t : t + 1], ALU.mult, ALU.add)
+
+        def new_variance(h):
+            cols = slice(h * HALF, (h + 1) * HALF)
+            for tp in range(2):
+                nc.vector.scalar_tensor_tensor(part(kick, h, tp), dw[h, tp][:], 0.2, part(vol, h, tp), ALU.mult, ALU.mult)
+            nc.vector.tensor_tensor(pre[:, :, cols], kick[:, :, cols], drift[:, :, cols], ALU.add)
+
+        def fetch_anti(h):
+            for t in range(PACK):
+                nc.scalar.activation(
+                    pre_anti[:, t, h * HALF : (h + 1) * HALF],
+                    pre[:, t, :].indirect(anti_sb[:, h * HALF // 16 : (h + 1) * HALF // 16]),
+                    ACT.Copy,
+                )
+
+        payoff = {}
+
+        def returns(c):
+            cols = slice(c * CHUNK, (c + 1) * CHUNK)
+            noise = sb([P, PACK, CHUNK], F32, f"noise{c}")
+            base = sb([P, PACK, CHUNK], F32, f"base{c}")
+            ret = sb([P, PACK, CHUNK], F32, f"ret{c}")
+            bent = sb([P, PACK, CHUNK], F32, f"bent{c}")
+            spot = sb([P, PACK, CHUNK], F32, f"spot{c}")
+            payoff[c] = sb([P, PACK, CHUNK], F32, f"payoff{c}")
+            nc.vector.tensor_tensor(noise[:], vol[:, :, cols], shock[:, :, cols], ALU.mult)
+            nc.vector.scalar_tensor_tensor(base[:], var[:, :, cols], 0.5, noise[:], ALU.mult, ALU.add)
+            nc.vector.scalar_tensor_tensor(ret[:], pre[:, :, cols], 0.0, base[:], ALU.max, ALU.add)
+            nc.scalar.activation(bent[:], ret[:], ACT.Tanh, scale=-0.5)
+            nc.scalar.activation(spot[:], bent[:], ACT.Exp, scale=0.9)
+            nc.scalar.activation(payoff[c][:], spot[:], ACT.Relu, bias=-0.8)
+
+        def claims(c):
+            cols = slice(c * CHUNK, (c + 1) * CHUNK)
+            gap = sb([P, PACK, CHUNK], F32, f"gap{c}")
+            hid = sb([P, CHUNK * PACK], BF16, f"hid{c}")
+            codes = sb([P, CHUNK], U32, f"codes{c}")
+            scales = sb([P, CHUNK], U8, f"scales{c}")
+            staged = sb([P, CHUNK], F32, f"staged{c}")
+            nc.vector.scalar_tensor_tensor(gap[:], pre_anti[:, :, cols], 0.0, payoff[c][:], ALU.max, ALU.subtract)
+            nc.vector.tensor_tensor(
+                hid[:].rearrange("p (g i t) -> p g t i", i=4, t=PACK),
+                gap[:].rearrange("p t (g i) -> p g t i", i=4),
+                neg_unit[:].rearrange("p (a t b) -> p a t b", a=1, b=1).to_broadcast([P, CHUNK // 4, PACK, 4]),
+                ALU.mult,
+            )
+            nc.vector.quantize_mx(out=codes[:].bitcast(FP8X4), scales=scales[:], in_=hid[:])
+            h, tp = banks[c]
+            acc = psum.tile([P, CHUNK], F32, name=f"acc{c}", tag=f"vv{h}{tp}")
+            nc.tensor.matmul_mx(
+                out=acc[:], lhsT=w3[:].bitcast(FP4X4), lhsT_scale=w3s[:], rhs=codes[:].bitcast(FP8X4), rhs_scale=scales[:], start=True, stop=True
+            )
+            nc.scalar.copy(staged[:], acc[:])
+            nc.sync.dma_start(out=out[:, cols], in_=staged[:])
+
+        new_variance(0)
+        returns(0)
+        new_variance(1)
+        returns(1)
+        fetch_anti(0)
+        returns(2)
+        claims(0)
+        fetch_anti(1)
+        returns(3)
+        claims(1)
+        claims(2)
+        claims(3)

@@ -29,6 +29,7 @@ def tile_picked_yhestm_call_p_kernel(
     nc = tc.nc
     with ExitStack() as ctx:
         keep = ctx.enter_context(tc.tile_pool(name="keep", bufs=1))
+        relay = ctx.enter_context(tc.tile_pool(name="relay", bufs=1))
         psum = ctx.enter_context(tc.psum_pool(name="psum", bufs=1))
 
         def sb(shape, dtype, name, tag=None):
@@ -37,10 +38,10 @@ def tile_picked_yhestm_call_p_kernel(
         offs_sb = keep.tile([P, S // 16], U16, name="offs_sb")
         anti_sb = keep.tile([P, S // 16], U16, name="anti_sb")
         xs = sb([P, PASSES, T], U8, "xs")
-        w1s_raw = sb([P, PASSES, H], U8, "w1s_raw")
+        w1s_raw = relay.tile([P, PASSES, H], U8, name="w1s_raw", align_bytes=64, offset=1792)
         w2s_raw = sb([P, PASSES, H], U8, "w2s_raw")
         nc.gpsimd.memset(xs[:].bitcast(I32), 0)
-        nc.vector.memset(w1s_raw[:].bitcast(I32), 0)
+        nc.gpsimd.memset(w1s_raw[:].bitcast(I32), 0)
         nc.vector.memset(w2s_raw[:].bitcast(I32), 0)
 
         def load_scales(queues, tile, dram):
@@ -58,8 +59,8 @@ def tile_picked_yhestm_call_p_kernel(
         nc.scalar.dma_start(out=w1_raw[:].bitcast(I32), in_=w1_words.rearrange("o p n -> p o n").bitcast(I32))
         nc.scalar.dma_start(out=xw[:].bitcast(I32), in_=x_words.rearrange("o p n t -> p o (n t)").bitcast(I32))
         nc.sync.dma_start(anti_sb[:], anti)
-        load_scales([nc.gpsimd, nc.gpsimd, nc.sync, nc.sync], w1s_raw, w1_scales)
-        load_scales([nc.gpsimd, nc.gpsimd, nc.sync, nc.sync], w2s_raw, w2_scales)
+        load_scales([nc.gpsimd, nc.sync, nc.sync, nc.sync], w1s_raw, w1_scales)
+        load_scales([nc.sync] * 4, w2s_raw, w2_scales)
 
         def deal_words(raw, name):
             dealt = sb([P, PASSES, 2 * H], U8, name)
@@ -77,15 +78,20 @@ def tile_picked_yhestm_call_p_kernel(
             )
             return dealt
 
-        gw = [[sb([P, HALF], U32, f"gw{h}{o}") for o in range(PASSES)] for h in range(2)]
-        gs = [[sb([P, HALF], U8, f"gs{h}{o}") for o in range(PASSES)] for h in range(2)]
+        gw, gs = {}, {}
 
         def gather_paths(h):
+            if h == 0:
+                gw[h] = sb([P, PASSES, HALF], U32, "gw0")
+                gs[h] = sb([P, PASSES, HALF], U8, "gs0")
+            else:
+                gw[h] = relay.tile([P, PASSES, HALF], U32, name="gw1", align_bytes=64, offset=0)
+                gs[h] = relay.tile([P, PASSES, HALF], U8, name="gs1", align_bytes=64, offset=2048)
             picked = offs_sb[:, h * HALF // 16 : (h + 1) * HALF // 16]
             for o in range(PASSES):
-                nc.vector.tensor_copy(gs[h][o][:], xs[:, o, :].indirect(picked))
+                nc.vector.tensor_copy(gs[h][:, o, :], xs[:, o, :].indirect(picked))
             for o in range(PASSES):
-                nc.vector.tensor_copy(gw[h][o][:], xw[:, o, :].indirect(picked))
+                nc.vector.tensor_copy(gw[h][:, o, :], xw[:, o, :].indirect(picked))
 
         def product(words, scales, h, tp, tag):
             bank = psum.tile([P, 2, HALF], F32, name=f"{tag}{h}{tp}", tag=f"{tag}{h}{tp}")
@@ -96,8 +102,8 @@ def tile_picked_yhestm_call_p_kernel(
                         out=bank[:, j, :],
                         lhsT=words[:, o, 2 * P * t : 2 * P * (t + 1)].bitcast(FP4X4),
                         lhsT_scale=scales[:, o, P * t : P * (t + 1)],
-                        rhs=gw[h][o][:].bitcast(FP8X4),
-                        rhs_scale=gs[h][o][:],
+                        rhs=gw[h][:, o, :].bitcast(FP8X4),
+                        rhs_scale=gs[h][:, o, :],
                         start=(o == 0),
                         stop=(o == PASSES - 1),
                     )
@@ -111,7 +117,7 @@ def tile_picked_yhestm_call_p_kernel(
         nc.sync.dma_start(out=w2_raw[:].bitcast(I32), in_=w2_words.rearrange("o p n -> p o n").bitcast(I32))
         w1s = deal_scales(w1s_raw, "w1s")
         gather_paths(0)
-        z2_sb = sb([P, PACK, S], F32, "z2_sb", tag="w1s_raw")
+        z2_sb = relay.tile([P, PACK, S], F32, name="z2_sb", align_bytes=64, offset=2560)
         nc.sync.dma_start(out=z2_sb[:], in_=z2.rearrange("(p t) n -> p t n", t=PACK))
         gather_paths(1)
         kap_sb = sb([P, PACK], F32, "kap_sb", tag="xs")
@@ -122,8 +128,8 @@ def tile_picked_yhestm_call_p_kernel(
         def plane(name):
             return sb([P, PACK, S], F32, name)
 
-        growth, capped, soft, var, drift, vol, shock, kick, pre, pre_anti = [
-            plane(n) for n in ("growth", "capped", "soft", "var", "drift", "vol", "shock", "kick", "pre", "pre_anti")
+        growth, capped, soft, var, vol, shock, kick, pre, half_new, hedge = [
+            plane(n) for n in ("growth", "capped", "soft", "var", "vol", "shock", "kick", "pre", "half_new", "hedge")
         ]
         banks = [(h, tp) for h in range(2) for tp in range(2)]
         vv, dw = {}, {}
@@ -141,10 +147,8 @@ def tile_picked_yhestm_call_p_kernel(
 
         half_keep = sb([P, PACK], F32, "half_keep")
         half_pull = sb([P, PACK], F32, "half_pull")
-        neg_unit = sb([P, PACK], F32, "neg_unit")
         nc.gpsimd.tensor_scalar(half_keep[:], kap_sb[:], -0.5, 0.5, ALU.mult, ALU.add)
         nc.gpsimd.tensor_scalar(half_pull[:], kap_sb[:], 0.35, 0.0, ALU.mult, ALU.add)
-        nc.gpsimd.tensor_scalar(neg_unit[:], unit_sb[:], -1.0, 0.0, ALU.mult, ALU.add)
 
         for h, tp in banks:
             dw[h, tp] = product(w2, w2s, h, tp, "dw")
@@ -155,75 +159,66 @@ def tile_picked_yhestm_call_p_kernel(
             nc.scalar.activation(soft[:, :, cols], capped[:, :, cols], ACT.Ln)
         for h, tp in banks:
             nc.vector.tensor_tensor(part(var, h, tp), vv[h, tp][:], part(soft, h, tp), ALU.max)
-        for h, tp in banks:
+        by_rows = [(h, tp) for tp in range(2) for h in range(2)]
+        for h, tp in by_rows:
             nc.scalar.activation(part(vol, h, tp), part(var, h, tp), ACT.Sqrt, bias=0.02)
-        for t in range(PACK):
-            if True:
-                nc.vector.tensor_scalar(drift[:, t, :], var[:, t, :], half_keep[:, t : t + 1], half_pull[:, t : t + 1], ALU.mult, ALU.add)
-
-        def new_variance(h):
-            cols = slice(h * HALF, (h + 1) * HALF)
-            for tp in range(2):
+        for tp in range(2):
+            for h in range(2):
                 nc.vector.scalar_tensor_tensor(part(kick, h, tp), dw[h, tp][:], 0.2, part(vol, h, tp), ALU.mult, ALU.mult)
-            nc.vector.tensor_tensor(pre[:, :, cols], kick[:, :, cols], drift[:, :, cols], ALU.add)
-
-        def fetch_anti(h):
-            for t in range(PACK):
+            for t in range(2 * tp, 2 * tp + 2):
+                nc.vector.scalar_tensor_tensor(pre[:, t, :], var[:, t, :], half_keep[:, t : t + 1], kick[:, t, :], ALU.mult, ALU.add)
+            for t in range(2 * tp, 2 * tp + 2):
+                if tp == 0:
+                    nc.scalar.activation(half_new[:, t, :], pre[:, t, :], ACT.Relu, bias=half_pull[:, t : t + 1])
+                else:
+                    nc.vector.tensor_scalar(half_new[:, t, :], pre[:, t, :], half_pull[:, t : t + 1], 0.0, ALU.add, ALU.max)
+        for t in range(PACK):
+            for h in range(2):
                 nc.scalar.activation(
-                    pre_anti[:, t, h * HALF : (h + 1) * HALF],
-                    pre[:, t, :].indirect(anti_sb[:, h * HALF // 16 : (h + 1) * HALF // 16]),
+                    hedge[:, t, h * HALF : (h + 1) * HALF],
+                    half_new[:, t, :].indirect(anti_sb[:, h * HALF // 16 : (h + 1) * HALF // 16]),
                     ACT.Copy,
+                    bias=0.8,
                 )
 
-        payoff = {}
+        chunks = S // CHUNK
+        cols = [slice(c * CHUNK, (c + 1) * CHUNK) for c in range(chunks)]
 
-        def returns(c):
-            cols = slice(c * CHUNK, (c + 1) * CHUNK)
-            noise = sb([P, PACK, CHUNK], F32, f"noise{c}")
-            base = sb([P, PACK, CHUNK], F32, f"base{c}")
-            ret = sb([P, PACK, CHUNK], F32, f"ret{c}")
-            bent = sb([P, PACK, CHUNK], F32, f"bent{c}")
-            spot = sb([P, PACK, CHUNK], F32, f"spot{c}")
-            payoff[c] = sb([P, PACK, CHUNK], F32, f"payoff{c}")
-            nc.vector.tensor_tensor(noise[:], vol[:, :, cols], shock[:, :, cols], ALU.mult)
-            nc.vector.scalar_tensor_tensor(base[:], var[:, :, cols], 0.5, noise[:], ALU.mult, ALU.add)
-            nc.vector.scalar_tensor_tensor(ret[:], pre[:, :, cols], 0.0, base[:], ALU.max, ALU.add)
-            nc.scalar.activation(bent[:], ret[:], ACT.Tanh, scale=-0.5)
-            nc.scalar.activation(spot[:], bent[:], ACT.Exp, scale=0.9)
-            nc.scalar.activation(payoff[c][:], spot[:], ACT.Relu, bias=-0.8)
+        def pieces(name, dtype=F32, shape=(P, PACK, CHUNK)):
+            return [sb(list(shape), dtype, f"{name}{c}") for c in range(chunks)]
 
-        def claims(c):
-            cols = slice(c * CHUNK, (c + 1) * CHUNK)
-            gap = sb([P, PACK, CHUNK], F32, f"gap{c}")
-            hid = sb([P, CHUNK * PACK], BF16, f"hid{c}")
-            codes = sb([P, CHUNK], U32, f"codes{c}")
-            scales = sb([P, CHUNK], U8, f"scales{c}")
-            staged = sb([P, CHUNK], F32, f"staged{c}")
-            nc.vector.scalar_tensor_tensor(gap[:], pre_anti[:, :, cols], 0.0, payoff[c][:], ALU.max, ALU.subtract)
-            nc.vector.tensor_tensor(
-                hid[:].rearrange("p (g i t) -> p g t i", i=4, t=PACK),
-                gap[:].rearrange("p t (g i) -> p g t i", i=4),
-                neg_unit[:].rearrange("p (a t b) -> p a t b", a=1, b=1).to_broadcast([P, CHUNK // 4, PACK, 4]),
-                ALU.mult,
-            )
-            nc.vector.quantize_mx(out=codes[:].bitcast(FP8X4), scales=scales[:], in_=hid[:])
-            h, tp = banks[c]
-            acc = psum.tile([P, CHUNK], F32, name=f"acc{c}", tag=f"vv{h}{tp}")
-            nc.tensor.matmul_mx(
-                out=acc[:], lhsT=w3[:].bitcast(FP4X4), lhsT_scale=w3s[:], rhs=codes[:].bitcast(FP8X4), rhs_scale=scales[:], start=True, stop=True
-            )
-            nc.scalar.copy(staged[:], acc[:])
-            nc.sync.dma_start(out=out[:, cols], in_=staged[:])
+        ret, bent, spot, gap = [pieces(n) for n in ("ret", "bent", "spot", "gap")]
+        noise, base = plane("noise"), plane("base")
+        hid = pieces("hid", BF16, (P, CHUNK * PACK))
+        codes = pieces("codes", U32, (P, CHUNK))
+        scales = pieces("scales", U8, (P, CHUNK))
+        staged = pieces("staged", F32, (P, CHUNK))
 
-        new_variance(0)
-        returns(0)
-        new_variance(1)
-        returns(1)
-        fetch_anti(0)
-        returns(2)
-        claims(0)
-        fetch_anti(1)
-        returns(3)
-        claims(1)
-        claims(2)
-        claims(3)
+        halves = [slice(h * HALF, (h + 1) * HALF) for h in range(2)]
+        for h in halves:
+            nc.vector.tensor_tensor(noise[:, :, h], vol[:, :, h], shock[:, :, h], ALU.mult)
+        for h in halves:
+            nc.vector.scalar_tensor_tensor(base[:, :, h], var[:, :, h], 0.5, noise[:, :, h], ALU.mult, ALU.add)
+        for c in range(chunks):
+            nc.vector.tensor_tensor(ret[c][:], half_new[:, :, cols[c]], base[:, :, cols[c]], ALU.add)
+            nc.scalar.activation(bent[c][:], ret[c][:], ACT.Tanh, scale=-0.5)
+            nc.scalar.activation(spot[c][:], bent[c][:], ACT.Exp, scale=0.9)
+        for pair in ((0, 1), (2, 3)):
+            for c in pair:
+                nc.vector.scalar_tensor_tensor(gap[c][:], spot[c][:], 0.8, hedge[:, :, cols[c]], ALU.max, ALU.subtract)
+            for c in pair:
+                nc.vector.tensor_tensor(
+                    hid[c][:].rearrange("p (g i t) -> p g t i", i=4, t=PACK),
+                    gap[c][:].rearrange("p t (g i) -> p g t i", i=4),
+                    unit_sb[:].rearrange("p (a t b) -> p a t b", a=1, b=1).to_broadcast([P, CHUNK // 4, PACK, 4]),
+                    ALU.mult,
+                )
+            for c in pair:
+                nc.vector.quantize_mx(out=codes[c][:].bitcast(FP8X4), scales=scales[c][:], in_=hid[c][:])
+                h, tp = banks[c]
+                acc = psum.tile([P, CHUNK], F32, name=f"acc{c}", tag=f"vv{h}{tp}")
+                nc.tensor.matmul_mx(
+                    out=acc[:], lhsT=w3[:].bitcast(FP4X4), lhsT_scale=w3s[:], rhs=codes[c][:].bitcast(FP8X4), rhs_scale=scales[c][:], start=True, stop=True
+                )
+                nc.scalar.copy(staged[c][:], acc[:])
+                nc.sync.dma_start(out=out[:, cols[c]], in_=staged[c][:])

@@ -1,6 +1,7 @@
 from contextlib import ExitStack
 
 import concourse.mybir as mybir
+from concourse.masks import make_identity
 
 K, T, S, N, H = 1024, 1024, 512, 128, 512
 FLOPS = 2 * (2 * K * H * S + H * N * S)
@@ -51,47 +52,49 @@ def tile_picked_yhestm_call_p_kernel(
                     in_=dram[:, 4 * q : 4 * q + 4, :].rearrange("o r n -> r o n").bitcast(I32),
                 )
 
-        xw = sb([P, PASSES, T], U32, "xw")
+        xw = [sb([P, T], U32, f"xw{o}") for o in range(PASSES)]
         w1_raw = sb([P, PASSES, 2 * H], U8, "w1_raw")
 
         nc.sync.dma_start(offs_sb[:], offs)
         load_scales([nc.sync] * 4, xs, x_scales)
         nc.scalar.dma_start(out=w1_raw[:].bitcast(I32), in_=w1_words.rearrange("o p n -> p o n").bitcast(I32))
-        nc.scalar.dma_start(out=xw[:].bitcast(I32), in_=x_words.rearrange("o p n t -> p o (n t)").bitcast(I32))
+        for o in range(PASSES):
+            nc.scalar.dma_start(out=xw[o][:].bitcast(I32), in_=x_words[o].rearrange("p n t -> p (n t)").bitcast(I32))
         nc.sync.dma_start(anti_sb[:], anti)
-        load_scales([nc.gpsimd, nc.sync, nc.sync, nc.sync], w1s_raw, w1_scales)
+        load_scales([nc.gpsimd, nc.gpsimd, nc.sync, nc.sync], w1s_raw, w1_scales)
         load_scales([nc.sync] * 4, w2s_raw, w2_scales)
 
         def deal_words(raw, name):
             dealt = sb([P, PASSES, 2 * H], U8, name)
             nc.vector.tensor_copy(
-                out=dealt[:].bitcast(U16).rearrange("p o (t m) -> p o t m", t=PACK),
-                in_=raw[:].bitcast(U16).rearrange("p o (m t) -> p o t m", t=PACK),
+                out=dealt[:].bitcast(U16).rearrange("p o (t g i) -> p o g t i", t=PACK, i=8),
+                in_=raw[:].bitcast(U16).rearrange("p o (g i t) -> p o g t i", t=PACK, i=8),
             )
             return dealt
 
         def deal_scales(raw, name):
             dealt = sb([P, PASSES, H], U8, name)
             nc.vector.tensor_copy(
-                out=dealt[:].rearrange("p o (t m) -> p o t m", t=PACK),
-                in_=raw[:].rearrange("p o (m t) -> p o t m", t=PACK),
+                out=dealt[:].rearrange("p o (t g i) -> p o g t i", t=PACK, i=16),
+                in_=raw[:].rearrange("p o (g i t) -> p o g t i", t=PACK, i=16),
             )
             return dealt
 
         gw, gs = {}, {}
 
         def gather_paths(h):
+            gw[h, 0] = sb([P, HALF], U32, f"gw{h}0")
             if h == 0:
-                gw[h] = sb([P, PASSES, HALF], U32, "gw0")
+                gw[h, 1] = sb([P, HALF], U32, "gw01")
                 gs[h] = sb([P, PASSES, HALF], U8, "gs0")
             else:
-                gw[h] = relay.tile([P, PASSES, HALF], U32, name="gw1", align_bytes=64, offset=0)
+                gw[h, 1] = relay.tile([P, HALF], U32, name="gw11", align_bytes=64, offset=1024)
                 gs[h] = relay.tile([P, PASSES, HALF], U8, name="gs1", align_bytes=64, offset=2048)
             picked = offs_sb[:, h * HALF // 16 : (h + 1) * HALF // 16]
             for o in range(PASSES):
                 nc.vector.tensor_copy(gs[h][:, o, :], xs[:, o, :].indirect(picked))
             for o in range(PASSES):
-                nc.vector.tensor_copy(gw[h][:, o, :], xw[:, o, :].indirect(picked))
+                nc.vector.tensor_copy(gw[h, o][:], xw[o][:].indirect(picked))
 
         def product(words, scales, h, tp, tag):
             bank = psum.tile([P, 2, HALF], F32, name=f"{tag}{h}{tp}", tag=f"{tag}{h}{tp}")
@@ -102,7 +105,7 @@ def tile_picked_yhestm_call_p_kernel(
                         out=bank[:, j, :],
                         lhsT=words[:, o, 2 * P * t : 2 * P * (t + 1)].bitcast(FP4X4),
                         lhsT_scale=scales[:, o, P * t : P * (t + 1)],
-                        rhs=gw[h][:, o, :].bitcast(FP8X4),
+                        rhs=gw[h, o][:].bitcast(FP8X4),
                         rhs_scale=gs[h][:, o, :],
                         start=(o == 0),
                         stop=(o == PASSES - 1),
@@ -121,7 +124,7 @@ def tile_picked_yhestm_call_p_kernel(
         nc.sync.dma_start(out=z2_sb[:], in_=z2.rearrange("(p t) n -> p t n", t=PACK))
         gather_paths(1)
         kap_sb = sb([P, PACK], F32, "kap_sb", tag="xs")
-        unit_sb = sb([P, PACK], F32, "unit_sb", tag="xw")
+        unit_sb = sb([P, PACK], F32, "unit_sb", tag="xw1")
         nc.sync.dma_start(out=kap_sb[:], in_=kap.rearrange("(p t) o -> p (t o)", t=PACK))
         nc.sync.dma_start(out=unit_sb[:], in_=unit.rearrange("(p t) o -> p (t o)", t=PACK))
 
@@ -148,7 +151,10 @@ def tile_picked_yhestm_call_p_kernel(
         half_keep = sb([P, PACK], F32, "half_keep")
         half_pull = sb([P, PACK], F32, "half_pull")
         nc.gpsimd.tensor_scalar(half_keep[:], kap_sb[:], -0.5, 0.5, ALU.mult, ALU.add)
-        nc.gpsimd.tensor_scalar(half_pull[:], kap_sb[:], 0.35, 0.0, ALU.mult, ALU.add)
+        nc.gpsimd.tensor_scalar(half_pull[:, 0:2], kap_sb[:, 0:2], 0.35, 0.0, ALU.mult, ALU.add)
+        nc.gpsimd.tensor_scalar(half_pull[:, 2:4], kap_sb[:, 2:4], 0.35, 0.8, ALU.mult, ALU.add)
+        ident = sb([P, P], F32, "ident")
+        make_identity(nc, ident[:])
 
         for h, tp in banks:
             dw[h, tp] = product(w2, w2s, h, tp, "dw")
@@ -162,63 +168,92 @@ def tile_picked_yhestm_call_p_kernel(
         by_rows = [(h, tp) for tp in range(2) for h in range(2)]
         for h, tp in by_rows:
             nc.scalar.activation(part(vol, h, tp), part(var, h, tp), ACT.Sqrt, bias=0.02)
+        chunks = S // CHUNK
+        cols = [slice(c * CHUNK, (c + 1) * CHUNK) for c in range(chunks)]
+        half_var, noise = plane("half_var"), plane("noise")
+        for tp in range(2):
+            rows = slice(2 * tp, 2 * tp + 2)
+            nc.vector.tensor_scalar(half_var[:, rows, :], var[:, rows, :], 0.5, -0.8 * tp, ALU.mult, ALU.add)
+        total = [psum.tile([P, PACK, P], F32, name=f"total{c}", tag="vv%d%d" % banks[c]) for c in range(chunks)]
+
+        def add_turned(c, source, start=False, stop=False):
+            for t in range(PACK):
+                nc.tensor.matmul(
+                    total[c][:, t, :], source[:, t, cols[c]], ident[:], start=start and t == 0, stop=stop and t == PACK - 1, is_transpose=True
+                )
+
+        for c in range(chunks):
+            add_turned(c, half_var, start=True)
+
+        def make_noise(c):
+            nc.vector.tensor_tensor(noise[:, :, cols[c]], vol[:, :, cols[c]], shock[:, :, cols[c]], ALU.mult)
+
         for tp in range(2):
             for h in range(2):
                 nc.vector.scalar_tensor_tensor(part(kick, h, tp), dw[h, tp][:], 0.2, part(vol, h, tp), ALU.mult, ALU.mult)
+            if tp == 1:
+                make_noise(0)
+                add_turned(0, noise)
             for t in range(2 * tp, 2 * tp + 2):
                 nc.vector.scalar_tensor_tensor(pre[:, t, :], var[:, t, :], half_keep[:, t : t + 1], kick[:, t, :], ALU.mult, ALU.add)
             for t in range(2 * tp, 2 * tp + 2):
                 if tp == 0:
                     nc.scalar.activation(half_new[:, t, :], pre[:, t, :], ACT.Relu, bias=half_pull[:, t : t + 1])
                 else:
-                    nc.vector.tensor_scalar(half_new[:, t, :], pre[:, t, :], half_pull[:, t : t + 1], 0.0, ALU.add, ALU.max)
-        for t in range(PACK):
-            for h in range(2):
-                nc.scalar.activation(
-                    hedge[:, t, h * HALF : (h + 1) * HALF],
-                    half_new[:, t, :].indirect(anti_sb[:, h * HALF // 16 : (h + 1) * HALF // 16]),
-                    ACT.Copy,
-                    bias=0.8,
-                )
+                    nc.vector.tensor_scalar(half_new[:, t, :], pre[:, t, :], half_pull[:, t : t + 1], 0.8, ALU.add, ALU.max)
 
-        chunks = S // CHUNK
-        cols = [slice(c * CHUNK, (c + 1) * CHUNK) for c in range(chunks)]
+        def fetch(t, h, on_vector=False):
+            fetched = hedge[:, t, h * HALF : (h + 1) * HALF]
+            window = half_new[:, t, :].indirect(anti_sb[:, h * HALF // 16 : (h + 1) * HALF // 16])
+            if on_vector:
+                nc.vector.tensor_copy(fetched, window)
+            else:
+                nc.scalar.activation(fetched, window, ACT.Copy, bias=0.8 if t < 2 else 0.0)
 
         def pieces(name, dtype=F32, shape=(P, PACK, CHUNK)):
             return [sb(list(shape), dtype, f"{name}{c}") for c in range(chunks)]
 
-        ret, bent, spot, gap = [pieces(n) for n in ("ret", "bent", "spot", "gap")]
-        noise, base = plane("noise"), plane("base")
+        spot, gap = [pieces(n) for n in ("spot", "gap")]
+        bent = [hedge[:, 2:4, HALF:]] + [sb([P, 2, HALF], F32, f"bent{c}")[:] for c in range(1, chunks)]
         hid = pieces("hid", BF16, (P, CHUNK * PACK))
         codes = pieces("codes", U32, (P, CHUNK))
         scales = pieces("scales", U8, (P, CHUNK))
         staged = pieces("staged", F32, (P, CHUNK))
+        back = {}
 
-        halves = [slice(h * HALF, (h + 1) * HALF) for h in range(2)]
-        for h in halves:
-            nc.vector.tensor_tensor(noise[:, :, h], vol[:, :, h], shock[:, :, h], ALU.mult)
-        for h in halves:
-            nc.vector.scalar_tensor_tensor(base[:, :, h], var[:, :, h], 0.5, noise[:, :, h], ALU.mult, ALU.add)
+        def returns(c):
+            add_turned(c, half_new, stop=c == 0)
+            if c > 0:
+                make_noise(c)
+                add_turned(c, noise, stop=True)
+            nc.scalar.activation(bent[c], total[c][:].rearrange("p (a t) m -> p a (t m)", a=2), ACT.Tanh, scale=-0.5)
+            nc.scalar.activation(spot[c][:].rearrange("p (a t) m -> p a (t m)", a=2), bent[c], ACT.Exp, scale=0.9)
+            back[c] = psum.tile([P, PACK, P], F32, name=f"back{c}", tag="dw%d%d" % banks[c])
+            for t in range(PACK):
+                nc.tensor.transpose(back[c][:, t, :], spot[c][:, t, :], ident[:])
+
+        for h in range(2):
+            for t in range(2):
+                fetch(t, h)
+        returns(0)
+        returns(1)
+        for t in range(2, PACK):
+            fetch(t, 0, on_vector=True)
+            fetch(t, 1)
+        returns(2)
+        returns(3)
         for c in range(chunks):
-            nc.vector.tensor_tensor(ret[c][:], half_new[:, :, cols[c]], base[:, :, cols[c]], ALU.add)
-            nc.scalar.activation(bent[c][:], ret[c][:], ACT.Tanh, scale=-0.5)
-            nc.scalar.activation(spot[c][:], bent[c][:], ACT.Exp, scale=0.9)
-        for pair in ((0, 1), (2, 3)):
-            for c in pair:
-                nc.vector.scalar_tensor_tensor(gap[c][:], spot[c][:], 0.8, hedge[:, :, cols[c]], ALU.max, ALU.subtract)
-            for c in pair:
-                nc.vector.tensor_tensor(
-                    hid[c][:].rearrange("p (g i t) -> p g t i", i=4, t=PACK),
-                    gap[c][:].rearrange("p t (g i) -> p g t i", i=4),
-                    unit_sb[:].rearrange("p (a t b) -> p a t b", a=1, b=1).to_broadcast([P, CHUNK // 4, PACK, 4]),
-                    ALU.mult,
-                )
-            for c in pair:
-                nc.vector.quantize_mx(out=codes[c][:].bitcast(FP8X4), scales=scales[c][:], in_=hid[c][:])
-                h, tp = banks[c]
-                acc = psum.tile([P, CHUNK], F32, name=f"acc{c}", tag=f"vv{h}{tp}")
-                nc.tensor.matmul_mx(
-                    out=acc[:], lhsT=w3[:].bitcast(FP4X4), lhsT_scale=w3s[:], rhs=codes[c][:].bitcast(FP8X4), rhs_scale=scales[c][:], start=True, stop=True
-                )
-                nc.scalar.copy(staged[c][:], acc[:])
-                nc.sync.dma_start(out=out[:, cols[c]], in_=staged[c][:])
+            nc.vector.scalar_tensor_tensor(gap[c][:], back[c][:], 0.8, hedge[:, :, cols[c]], ALU.max, ALU.subtract)
+            nc.vector.tensor_tensor(
+                hid[c][:].rearrange("p (g i t) -> p g t i", i=4, t=PACK),
+                gap[c][:].rearrange("p t (g i) -> p g t i", i=4),
+                unit_sb[:].rearrange("p (a t b) -> p a t b", a=1, b=1).to_broadcast([P, CHUNK // 4, PACK, 4]),
+                ALU.mult,
+            )
+            nc.vector.quantize_mx(out=codes[c][:].bitcast(FP8X4), scales=scales[c][:], in_=hid[c][:])
+            acc = psum.tile([P, CHUNK], F32, name=f"acc{c}", tag="vv%d%d" % banks[c])
+            nc.tensor.matmul_mx(
+                out=acc[:], lhsT=w3[:].bitcast(FP4X4), lhsT_scale=w3s[:], rhs=codes[c][:].bitcast(FP8X4), rhs_scale=scales[c][:], start=True, stop=True
+            )
+            nc.scalar.copy(staged[c][:], acc[:])
+            nc.sync.dma_start(out=out[:, cols[c]], in_=staged[c][:])

@@ -171,9 +171,8 @@ def tile_picked_yhestm_call_p_kernel(
         chunks = S // CHUNK
         cols = [slice(c * CHUNK, (c + 1) * CHUNK) for c in range(chunks)]
         half_var, noise = plane("half_var"), plane("noise")
-        for tp in range(2):
-            rows = slice(2 * tp, 2 * tp + 2)
-            nc.vector.tensor_scalar(half_var[:, rows, :], var[:, rows, :], 0.5, -0.8 * tp, ALU.mult, ALU.add)
+        for h, tp in banks:
+            nc.gpsimd.tensor_scalar(part(half_var, h, tp), part(var, h, tp), 0.5, -0.8 * tp, ALU.mult, ALU.add)
         total = [psum.tile([P, PACK, P], F32, name=f"total{c}", tag="vv%d%d" % banks[c]) for c in range(chunks)]
 
         def add_turned(c, source, start=False, stop=False):
@@ -191,9 +190,6 @@ def tile_picked_yhestm_call_p_kernel(
         for tp in range(2):
             for h in range(2):
                 nc.vector.scalar_tensor_tensor(part(kick, h, tp), dw[h, tp][:], 0.2, part(vol, h, tp), ALU.mult, ALU.mult)
-            if tp == 1:
-                make_noise(0)
-                add_turned(0, noise)
             for t in range(2 * tp, 2 * tp + 2):
                 nc.vector.scalar_tensor_tensor(pre[:, t, :], var[:, t, :], half_keep[:, t : t + 1], kick[:, t, :], ALU.mult, ALU.add)
             for t in range(2 * tp, 2 * tp + 2):
@@ -214,32 +210,33 @@ def tile_picked_yhestm_call_p_kernel(
             return [sb(list(shape), dtype, f"{name}{c}") for c in range(chunks)]
 
         spot, gap = [pieces(n) for n in ("spot", "gap")]
-        bent = [hedge[:, 2:4, HALF:]] + [sb([P, 2, HALF], F32, f"bent{c}")[:] for c in range(1, chunks)]
+        bent = [hedge[:, 1:3, HALF:]] + [sb([P, 2, HALF], F32, f"bent{c}")[:] for c in range(1, chunks)]
         hid = pieces("hid", BF16, (P, CHUNK * PACK))
         codes = pieces("codes", U32, (P, CHUNK))
         scales = pieces("scales", U8, (P, CHUNK))
-        staged = pieces("staged", F32, (P, CHUNK))
+        staged = [bent[-1][:, c // 2, (c % 2) * CHUNK : (c % 2 + 1) * CHUNK] for c in range(chunks)]
         back = {}
 
         def returns(c):
-            add_turned(c, half_new, stop=c == 0)
-            if c > 0:
-                make_noise(c)
-                add_turned(c, noise, stop=True)
+            add_turned(c, half_new)
+            make_noise(c)
+            add_turned(c, noise, stop=True)
             nc.scalar.activation(bent[c], total[c][:].rearrange("p (a t) m -> p a (t m)", a=2), ACT.Tanh, scale=-0.5)
             nc.scalar.activation(spot[c][:].rearrange("p (a t) m -> p a (t m)", a=2), bent[c], ACT.Exp, scale=0.9)
             back[c] = psum.tile([P, PACK, P], F32, name=f"back{c}", tag="dw%d%d" % banks[c])
             for t in range(PACK):
                 nc.tensor.transpose(back[c][:, t, :], spot[c][:, t, :], ident[:])
 
-        for h in range(2):
-            for t in range(2):
-                fetch(t, h)
+        fetch(0, 0)
+        fetch(1, 0)
+        fetch(0, 1)
         returns(0)
         returns(1)
-        for t in range(2, PACK):
-            fetch(t, 0, on_vector=True)
-            fetch(t, 1)
+        fetch(2, 0, on_vector=True)
+        fetch(3, 0, on_vector=True)
+        fetch(3, 1, on_vector=True)
+        fetch(1, 1)
+        fetch(2, 1)
         returns(2)
         returns(3)
         for c in range(chunks):
@@ -255,5 +252,5 @@ def tile_picked_yhestm_call_p_kernel(
             nc.tensor.matmul_mx(
                 out=acc[:], lhsT=w3[:].bitcast(FP4X4), lhsT_scale=w3s[:], rhs=codes[c][:].bitcast(FP8X4), rhs_scale=scales[c][:], start=True, stop=True
             )
-            nc.scalar.copy(staged[c][:], acc[:])
-            nc.sync.dma_start(out=out[:, cols[c]], in_=staged[c][:])
+            nc.scalar.copy(staged[c], acc[:])
+            nc.sync.dma_start(out=out[:, cols[c]], in_=staged[c])

from contextlib import ExitStack

import concourse.mybir as mybir
from concourse.masks import make_identity

K, T, S, N, H = 1024, 1024, 512, 128, 512
FLOPS = 2 * (2 * K * H * S + H * N * S)

F32 = mybir.dt.float32
BF16 = mybir.dt.bfloat16
I32 = mybir.dt.int32
U32 = mybir.dt.uint32
U16 = mybir.dt.uint16
U8 = mybir.dt.uint8
FP8X4 = mybir.dt.float8_e4m3fn_x4
FP4X4 = mybir.dt.float4_e2m1fn_x4
ALU = mybir.AluOpType
ACT = mybir.ActivationFunctionType

P = 128
PACK = 4
PASSES = K // (P * PACK)
HALF = S // 2
CHUNK = 128


def tile_picked_yhestm_call_p_kernel(
    tc, x_words, x_scales, w1_words, w1_scales, w2_words, w2_scales, kap, z2, unit, w3_words, w3_scales, offs, anti, out
):
    nc = tc.nc
    with ExitStack() as ctx:
        keep = ctx.enter_context(tc.tile_pool(name="keep", bufs=1))
        relay = ctx.enter_context(tc.tile_pool(name="relay", bufs=1))
        psum = ctx.enter_context(tc.psum_pool(name="psum", bufs=1))

        def sb(shape, dtype, name, tag=None):
            return keep.tile(shape, dtype, name=name, tag=tag or name, align_bytes=64)

        offs_sb = keep.tile([P, S // 16], U16, name="offs_sb")
        anti_sb = keep.tile([P, S // 16], U16, name="anti_sb")
        xs = sb([P, PASSES, T], U8, "xs")
        w1s_raw = relay.tile([P, PASSES, H], U8, name="w1s_raw", align_bytes=64, offset=1792)
        w2s_raw = sb([P, PASSES, H], U8, "w2s_raw")
        nc.gpsimd.memset(xs[:].bitcast(I32), 0)
        nc.gpsimd.memset(w1s_raw[:].bitcast(I32), 0)
        nc.vector.memset(w2s_raw[:].bitcast(I32), 0)

        def load_scales(queues, tile, dram):
            for q, queue in enumerate(queues):
                queue.dma_start(
                    out=tile[32 * q : 32 * q + 4, :, :].bitcast(I32),
                    in_=dram[:, 4 * q : 4 * q + 4, :].rearrange("o r n -> r o n").bitcast(I32),
                )

        xw = [sb([P, T], U32, f"xw{o}") for o in range(PASSES)]
        w1_raw = sb([P, PASSES, 2 * H], U8, "w1_raw")

        nc.sync.dma_start(offs_sb[:], offs)
        load_scales([nc.sync] * 4, xs, x_scales)
        nc.scalar.dma_start(out=w1_raw[:].bitcast(I32), in_=w1_words.rearrange("o p n -> p o n").bitcast(I32))
        for o in range(PASSES):
            nc.scalar.dma_start(out=xw[o][:].bitcast(I32), in_=x_words[o].rearrange("p n t -> p (n t)").bitcast(I32))
        nc.sync.dma_start(anti_sb[:], anti)
        load_scales([nc.gpsimd, nc.gpsimd, nc.sync, nc.sync], w1s_raw, w1_scales)
        load_scales([nc.sync] * 4, w2s_raw, w2_scales)

        def deal_words(raw, name):
            dealt = sb([P, PASSES, 2 * H], U8, name)
            nc.vector.tensor_copy(
                out=dealt[:].bitcast(U16).rearrange("p o (t g i) -> p o g t i", t=PACK, i=8),
                in_=raw[:].bitcast(U16).rearrange("p o (g i t) -> p o g t i", t=PACK, i=8),
            )
            return dealt

        def deal_scales(raw, name):
            dealt = sb([P, PASSES, H], U8, name)
            nc.vector.tensor_copy(
                out=dealt[:].rearrange("p o (t g i) -> p o g t i", t=PACK, i=16),
                in_=raw[:].rearrange("p o (g i t) -> p o g t i", t=PACK, i=16),
            )
            return dealt

        gw, gs = {}, {}

        def gather_paths(h):
            gw[h, 0] = sb([P, HALF], U32, f"gw{h}0")
            if h == 0:
                gw[h, 1] = sb([P, HALF], U32, "gw01")
                gs[h] = sb([P, PASSES, HALF], U8, "gs0")
            else:
                gw[h, 1] = relay.tile([P, HALF], U32, name="gw11", align_bytes=64, offset=1024)
                gs[h] = relay.tile([P, PASSES, HALF], U8, name="gs1", align_bytes=64, offset=2048)
            picked = offs_sb[:, h * HALF // 16 : (h + 1) * HALF // 16]
            for o in range(PASSES):
                nc.vector.tensor_copy(gs[h][:, o, :], xs[:, o, :].indirect(picked))
            for o in range(PASSES):
                nc.vector.tensor_copy(gw[h, o][:], xw[o][:].indirect(picked))

        def product(words, scales, h, tp, tag):
            bank = psum.tile([P, 2, HALF], F32, name=f"{tag}{h}{tp}", tag=f"{tag}{h}{tp}")
            for j in range(2):
                t = 2 * tp + j
                for o in range(PASSES):
                    nc.tensor.matmul_mx(
                        out=bank[:, j, :],
                        lhsT=words[:, o, 2 * P * t : 2 * P * (t + 1)].bitcast(FP4X4),
                        lhsT_scale=scales[:, o, P * t : P * (t + 1)],
                        rhs=gw[h, o][:].bitcast(FP8X4),
                        rhs_scale=gs[h][:, o, :],
                        start=(o == 0),
                        stop=(o == PASSES - 1),
                    )
            return bank

        def part(tile, h, tp):
            return tile[:, 2 * tp : 2 * tp + 2, h * HALF : (h + 1) * HALF]

        w1 = deal_words(w1_raw, "w1")
        w2_raw = sb([P, PASSES, 2 * H], U8, "w2_raw", tag="w1_raw")
        nc.sync.dma_start(out=w2_raw[:].bitcast(I32), in_=w2_words.rearrange("o p n -> p o n").bitcast(I32))
        w1s = deal_scales(w1s_raw, "w1s")
        gather_paths(0)
        z2_sb = relay.tile([P, PACK, S], F32, name="z2_sb", align_bytes=64, offset=2560)
        nc.sync.dma_start(out=z2_sb[:], in_=z2.rearrange("(p t) n -> p t n", t=PACK))
        gather_paths(1)
        kap_sb = sb([P, PACK], F32, "kap_sb", tag="xs")
        unit_sb = sb([P, PACK], F32, "unit_sb", tag="xw1")
        nc.sync.dma_start(out=kap_sb[:], in_=kap.rearrange("(p t) o -> p (t o)", t=PACK))
        nc.sync.dma_start(out=unit_sb[:], in_=unit.rearrange("(p t) o -> p (t o)", t=PACK))

        def plane(name):
            return sb([P, PACK, S], F32, name)

        growth, capped, soft, var, vol, shock, kick, pre, half_new, hedge = [
            plane(n) for n in ("growth", "capped", "soft", "var", "vol", "shock", "kick", "pre", "half_new", "hedge")
        ]
        banks = [(h, tp) for h in range(2) for tp in range(2)]
        vv, dw = {}, {}
        for h, tp in banks:
            vv[h, tp] = product(w1, w1s, h, tp, "vv")
            nc.scalar.activation(part(growth, h, tp), vv[h, tp][:], ACT.Exp)
        w2 = deal_words(w2_raw, "w2")
        w2s = deal_scales(w2s_raw, "w2s")
        w3 = sb([P, 2 * N], U8, "w3", tag="w1_raw")
        w3s = sb([P, N], U8, "w3s", tag="w2s_raw")
        nc.gpsimd.memset(w3s[:].bitcast(I32), 0)
        nc.sync.dma_start(out=w3[:].bitcast(I32), in_=w3_words[0].bitcast(I32))
        for q in range(4):
            nc.sync.dma_start(out=w3s[32 * q : 32 * q + 4, :].bitcast(I32), in_=w3_scales[0, 4 * q : 4 * q + 4, :].bitcast(I32))

        half_keep = sb([P, PACK], F32, "half_keep")
        half_pull = sb([P, PACK], F32, "half_pull")
        nc.gpsimd.tensor_scalar(half_keep[:], kap_sb[:], -0.5, 0.5, ALU.mult, ALU.add)
        nc.gpsimd.tensor_scalar(half_pull[:, 0:2], kap_sb[:, 0:2], 0.35, 0.0, ALU.mult, ALU.add)
        nc.gpsimd.tensor_scalar(half_pull[:, 2:4], kap_sb[:, 2:4], 0.35, 0.8, ALU.mult, ALU.add)
        ident = sb([P, P], F32, "ident")
        make_identity(nc, ident[:])

        for h, tp in banks:
            dw[h, tp] = product(w2, w2s, h, tp, "dw")
            nc.vector.scalar_tensor_tensor(part(shock, h, tp), part(z2_sb, h, tp), -2.0, dw[h, tp][:], ALU.mult, ALU.add)
        nc.vector.tensor_scalar(capped[:], growth[:], 2.0**60, 1.0, ALU.min, ALU.add)
        for h in range(2):
            cols = slice(h * HALF, (h + 1) * HALF)
            nc.scalar.activation(soft[:, :, cols], capped[:, :, cols], ACT.Ln)
        for h, tp in banks:
            nc.vector.tensor_tensor(part(var, h, tp), vv[h, tp][:], part(soft, h, tp), ALU.max)
        by_rows = [(h, tp) for tp in range(2) for h in range(2)]
        for h, tp in by_rows:
            nc.scalar.activation(part(vol, h, tp), part(var, h, tp), ACT.Sqrt, bias=0.02)
        chunks = S // CHUNK
        cols = [slice(c * CHUNK, (c + 1) * CHUNK) for c in range(chunks)]
        half_var, noise = plane("half_var"), plane("noise")
        for h, tp in banks:
            nc.gpsimd.tensor_scalar(part(half_var, h, tp), part(var, h, tp), 0.5, -0.8 * tp, ALU.mult, ALU.add)
        total = [psum.tile([P, PACK, P], F32, name=f"total{c}", tag="vv%d%d" % banks[c]) for c in range(chunks)]

        def add_turned(c, source, start=False, stop=False):
            for t in range(PACK):
                nc.tensor.matmul(
                    total[c][:, t, :], source[:, t, cols[c]], ident[:], start=start and t == 0, stop=stop and t == PACK - 1, is_transpose=True
                )

        for c in range(chunks):
            add_turned(c, half_var, start=True)

        def make_noise(c):
            nc.vector.tensor_tensor(noise[:, :, cols[c]], vol[:, :, cols[c]], shock[:, :, cols[c]], ALU.mult)

        for tp in range(2):
            for h in range(2):
                nc.vector.scalar_tensor_tensor(part(kick, h, tp), dw[h, tp][:], 0.2, part(vol, h, tp), ALU.mult, ALU.mult)
            for t in range(2 * tp, 2 * tp + 2):
                nc.vector.scalar_tensor_tensor(pre[:, t, :], var[:, t, :], half_keep[:, t : t + 1], kick[:, t, :], ALU.mult, ALU.add)
            for t in range(2 * tp, 2 * tp + 2):
                if tp == 0:
                    nc.scalar.activation(half_new[:, t, :], pre[:, t, :], ACT.Relu, bias=half_pull[:, t : t + 1])
                else:
                    nc.vector.tensor_scalar(half_new[:, t, :], pre[:, t, :], half_pull[:, t : t + 1], 0.8, ALU.add, ALU.max)

        def fetch(t, h, on_vector=False):
            fetched = hedge[:, t, h * HALF : (h + 1) * HALF]
            window = half_new[:, t, :].indirect(anti_sb[:, h * HALF // 16 : (h + 1) * HALF // 16])
            if on_vector:
                nc.vector.tensor_copy(fetched, window)
            else:
                nc.scalar.activation(fetched, window, ACT.Copy, bias=0.8 if t < 2 else 0.0)

        def pieces(name, dtype=F32, shape=(P, PACK, CHUNK)):
            return [sb(list(shape), dtype, f"{name}{c}") for c in range(chunks)]

        spot, gap = [pieces(n) for n in ("spot", "gap")]
        bent = [hedge[:, 1:3, HALF:]] + [sb([P, 2, HALF], F32, f"bent{c}")[:] for c in range(1, chunks)]
        hid = pieces("hid", BF16, (P, CHUNK * PACK))
        codes = pieces("codes", U32, (P, CHUNK))
        scales = pieces("scales", U8, (P, CHUNK))
        staged = [bent[-1][:, c // 2, (c % 2) * CHUNK : (c % 2 + 1) * CHUNK] for c in range(chunks)]
        back = {}

        def returns(c):
            add_turned(c, half_new)
            make_noise(c)
            add_turned(c, noise, stop=True)
            nc.scalar.activation(bent[c], total[c][:].rearrange("p (a t) m -> p a (t m)", a=2), ACT.Tanh, scale=-0.5)
            nc.scalar.activation(spot[c][:].rearrange("p (a t) m -> p a (t m)", a=2), bent[c], ACT.Exp, scale=0.9)
            back[c] = psum.tile([P, PACK, P], F32, name=f"back{c}", tag="dw%d%d" % banks[c])
            for t in range(PACK):
                nc.tensor.transpose(back[c][:, t, :], spot[c][:, t, :], ident[:])

        fetch(0, 0)
        fetch(1, 0)
        fetch(0, 1)
        returns(0)
        returns(1)
        fetch(2, 0, on_vector=True)
        fetch(3, 0, on_vector=True)
        fetch(3, 1, on_vector=True)
        fetch(1, 1)
        fetch(2, 1)
        returns(2)
        returns(3)
        for c in range(chunks):
            nc.vector.scalar_tensor_tensor(gap[c][:], back[c][:], 0.8, hedge[:, :, cols[c]], ALU.max, ALU.subtract)
            nc.vector.tensor_tensor(
                hid[c][:].rearrange("p (g i t) -> p g t i", i=4, t=PACK),
                gap[c][:].rearrange("p t (g i) -> p g t i", i=4),
                unit_sb[:].rearrange("p (a t b) -> p a t b", a=1, b=1).to_broadcast([P, CHUNK // 4, PACK, 4]),
                ALU.mult,
            )
            nc.vector.quantize_mx(out=codes[c][:].bitcast(FP8X4), scales=scales[c][:], in_=hid[c][:])
            acc = psum.tile([P, CHUNK], F32, name=f"acc{c}", tag="vv%d%d" % banks[c])
            nc.tensor.matmul_mx(
                out=acc[:], lhsT=w3[:].bitcast(FP4X4), lhsT_scale=w3s[:], rhs=codes[c][:].bitcast(FP8X4), rhs_scale=scales[c][:], start=True, stop=True
            )
            nc.scalar.copy(staged[c], acc[:])
            nc.sync.dma_start(out=out[:, cols[c]], in_=staged[c])
